import numpy as np
import ml_dtypes


def mxq(x, axis, fmt="e4m3"):
    dtype, down = {"e4m3": (ml_dtypes.float8_e4m3fn, 7), "e5m2": (ml_dtypes.float8_e5m2, 14)}[fmt]
    v = np.moveaxis(np.asarray(x, np.float32).astype(ml_dtypes.bfloat16).astype(np.float64), axis, -1)
    blocks = v.reshape(v.shape[:-1] + (-1, 32))
    amax = np.abs(blocks).max(-1, keepdims=True)
    byte = np.maximum(np.where(amax > 0, np.frexp(amax)[1] - 1 + 127, 0) - down, 1)
    scale = np.exp2(byte - 127.0)
    codes = (blocks / scale).astype(np.float32).astype(dtype).astype(np.float64)
    return np.moveaxis((codes * scale).reshape(v.shape), -1, axis)


WIDE = False


def mx_kscale(k):
    if not WIDE:
        return np.ones(k)
    levels = np.array([10, -10, 5, -5, 0])
    if k % 512:
        return np.exp2(np.random.permutation(np.resize(levels, k // 32))).repeat(32)
    a = np.empty((k // 512, 16))
    for p in range(k // 512):
        a[p, :8] = np.random.permutation(np.resize(levels, 8))
        for g in range(8):
            far = levels[np.abs(levels - a[p, g]) >= 10]
            a[p, g + 8] = far[np.random.randint(len(far))]
    return np.exp2(a.ravel()).repeat(32)


def f64(x):
    return np.asarray(x).astype(np.float64)


E2M1 = np.array([0.0, 0.5, 1.0, 1.5, 2.0, 3.0, 4.0, 6.0, -0.0, -0.5, -1.0, -1.5, -2.0, -3.0, -4.0, -6.0])


def pack_weight(w, fmt):
    k, n = w.shape
    w = f64(np.asarray(w, np.float32).astype(ml_dtypes.bfloat16)).reshape(k // 32, 32, n)
    amax = np.abs(w).max(1)
    if fmt == "e4m3":
        byte = np.frexp(amax)[1] - 1 + 127 - 7
    else:
        mant, ex = np.frexp(amax / 6.0)
        byte = np.where(mant > 0.5, ex, ex - 1) + 127
    byte = np.clip(np.where(amax > 0, byte, 1), 1, 254)
    scaled = (w * np.exp2(127.0 - byte)[:, None, :]).reshape(k, n).astype(np.float32)
    by_word = np.ascontiguousarray(scaled.reshape(k // 512, 128, 4, n).transpose(0, 1, 3, 2))
    if fmt == "e4m3":
        words = by_word.astype(ml_dtypes.float8_e4m3fn).view(np.uint8)
    else:
        c = by_word.astype(ml_dtypes.float4_e2m1fn).view(np.uint8) & 0xF
        words = (c[..., 0::2] | (c[..., 1::2] << 4)).reshape(k // 512, 128, 2 * n)
    return np.ascontiguousarray(words), np.ascontiguousarray(byte.astype(np.uint8).reshape(k // 512, 16, n))


def unpack_weight(words, scales, fmt):
    g, _, n = scales.shape
    words = np.ascontiguousarray(words).reshape(g, 128, n, -1)
    if fmt == "e4m3":
        vals = words.view(ml_dtypes.float8_e4m3fn).astype(np.float64)
    else:
        nib = np.empty((g, 128, n, 4), np.uint8)
        nib[..., 0::2] = words & 0xF
        nib[..., 1::2] = words >> 4
        vals = E2M1[nib]
    vals = vals * np.repeat(np.exp2(scales.astype(np.float64) - 127.0), 8, axis=1)[..., None]
    return vals.transpose(0, 1, 3, 2).reshape(g * 512, n)


K, T, S, N, M = 1024, 512, 512, 512, 512


def setup_inputs():
    n = np.random.standard_normal
    fk = mx_kscale(K)
    ft = mx_kscale(T)
    fs = mx_kscale(S)
    xtp = pack_weight(n((K, T)) / fk[:, None], "e4m3")
    wap = pack_weight(n((K, N)) * 1 / np.sqrt(K) * fk[:, None], "e2m1")
    wbp = pack_weight(n((K, M)) * 1 / np.sqrt(K) * fk[:, None], "e4m3")
    sap = pack_weight(n((S, N)) * fs[:, None], "e2m1")
    sbp = pack_weight(n((S, M)) / fs[:, None], "e4m3")
    return {
        "xt_words": xtp[0],
        "xt_scales": xtp[1],
        "wa_words": wap[0],
        "wa_scales": wap[1],
        "wb_words": wbp[0],
        "wb_scales": wbp[1],
        "ra": (np.random.uniform(0.5, 1.5, (1, T)) * ft).astype(np.float32),
        "rb": (np.random.uniform(0.5, 1.5, (1, T)) / ft).astype(np.float32),
        "sa_words": sap[0],
        "sa_scales": sap[1],
        "sb_words": sbp[0],
        "sb_scales": sbp[1],
    }


def reference(xt_words, xt_scales, wa_words, wa_scales, wb_words, wb_scales, ra, rb, sa_words, sa_scales, sb_words, sb_scales):
    xtu = unpack_weight(xt_words, xt_scales, "e4m3")
    wau = unpack_weight(wa_words, wa_scales, "e2m1")
    wbu = unpack_weight(wb_words, wb_scales, "e4m3")
    sau = unpack_weight(sa_words, sa_scales, "e2m1")
    sbu = unpack_weight(sb_words, sb_scales, "e4m3")
    a = wau.T @ xtu
    b = wbu.T @ xtu
    aw = np.maximum(a, 0.0) * f64(ra)
    bw = b * f64(rb)
    at = aw.T
    bt = bw.T
    atq = mxq(at, 0, "e4m3")
    btq = mxq(bt, 0, "e4m3")
    v = atq.T @ btq + sau.T @ sbu
    y = 0.04 * v
    return y

@@ -1,0 +1,247 @@
+from contextlib import ExitStack
+
+import concourse.mybir as mybir
+
+K, T, S, N, M = 1024, 512, 512, 512, 512
+FLOPS = 2 * K * T * N + 2 * K * T * M + 2 * T * N * M + 2 * S * N * M
+
+F32 = mybir.dt.float32
+BF16 = mybir.dt.bfloat16
+I32 = mybir.dt.int32
+U32 = mybir.dt.uint32
+U8 = mybir.dt.uint8
+FP8X4 = mybir.dt.float8_e4m3fn_x4
+FP4X4 = mybir.dt.float4_e2m1fn_x4
+ALU = mybir.AluOpType
+ACT = mybir.ActivationFunctionType
+AXIS = mybir.AxisListType
+
+P = 128
+PACK = 4
+PASSES = 2
+QUADS = 4
+CHUNK = 128
+CHUNKS = 4
+RUN = 8
+BLOCK = 32
+OUT_SCALE = 0.04
+PLANE_WORDS = 128
+
+
+def tile_mix_moment_of_two_layers_kernel(
+    tc, xt_words, xt_scales, wa_words, wa_scales, wb_words, wb_scales, ra, rb,
+    sa_words, sa_scales, sb_words, sb_scales, out,
+):
+    nc = tc.nc
+    with ExitStack() as ctx:
+        sb = ctx.enter_context(tc.tile_pool(name="sb", bufs=1))
+        ps = ctx.enter_context(tc.psum_pool(name="ps", bufs=1))
+        ctx.enter_context(tc.manual_schedule())
+
+        def sbuf(name, shape, dtype):
+            return sb.tile(shape, dtype, name=name, align_bytes=64)
+
+        def bank(index, shape):
+            return ps.tile(shape, F32, name="bank%d" % index)
+
+        x_raw = [sbuf("x_raw%d" % z, [P, T], U32) for z in range(PASSES)]
+        x_codes = [[sbuf("x_codes%d_%d" % (z, j), [P, P], U32) for j in range(PACK)] for z in range(PASSES)]
+        xs_stage = [sbuf("xs_stage%d" % z, [PACK, QUADS, PLANE_WORDS], I32) for z in range(PASSES)]
+        x_plane = [sbuf("x_plane%d" % z, [P, PLANE_WORDS], I32) for z in range(PASSES)]
+        wb_codes = [sbuf("wb_codes%d" % z, [P, M], U32) for z in range(PASSES)]
+        wbs_stage = [sbuf("wbs_stage%d" % z, [PACK, QUADS, PLANE_WORDS], I32) for z in range(PASSES)]
+        wb_plane = [sbuf("wb_plane%d" % z, [P, PLANE_WORDS], I32) for z in range(PASSES)]
+        wa_codes = sbuf("wa_codes", [P, PASSES, 2 * N], U8)
+        wa_plane = sbuf("wa_plane", [P, PASSES, N], U8)
+        sa_codes = sbuf("sa_codes", [P, 2 * N], U8)
+        sa_plane = sbuf("sa_plane", [P, N], U8)
+        sb_codes = sbuf("sb_codes", [P, M], U32)
+        sb_plane = sbuf("sb_plane", [P, M], U8)
+        r_block = sbuf("r_block", [P, 2, BLOCK], F32)
+        lane = sbuf("lane", [P, 2 * BLOCK], I32)
+        lane_low = sbuf("lane_low", [P, 2 * BLOCK], I32)
+        r_picked = sbuf("r_picked", [P, 2 * PACK, RUN], F32)
+        r_own = sbuf("r_own", [P, 2, PACK], F32)
+        at = [sbuf("at%d" % c, [P, CHUNK, PACK], BF16) for c in range(CHUNKS)]
+        bt = [sbuf("bt%d" % h, [P, 2 * CHUNK, PACK], BF16) for h in range(2)]
+        at_codes = [sbuf("at_codes%d" % c, [P, CHUNK], U32) for c in range(CHUNKS)]
+        at_plane = [sbuf("at_plane%d" % c, [P, CHUNK], U8) for c in range(CHUNKS)]
+        bt_codes = sbuf("bt_codes", [P, M], U32)
+        bt_plane = sbuf("bt_plane", [P, M], U8)
+
+        for z in range(PASSES):
+            nc.vector.memset(x_plane[z][:], 0)
+            nc.vector.memset(wb_plane[z][:], 0)
+        nc.vector.memset(wa_plane[:].bitcast(I32), 0)
+        nc.vector.memset(sa_plane[:].bitcast(I32), 0)
+        nc.vector.memset(sb_plane[:].bitcast(I32), 0)
+        nc.gpsimd.iota(lane[:], pattern=[[0, 2 * PACK], [-1, RUN]], base=RUN, channel_multiplier=1)
+
+        def fp8_words(words, z):
+            return words[z].rearrange("p n t -> p (n t)").bitcast(I32)
+
+        def staged_rows(scales, z):
+            return scales[z].bitcast(I32).rearrange("(q r) w -> r q w", r=PACK)
+
+        def load_plane(plane, scales):
+            rows = scales.bitcast(I32).rearrange("z (q r) w -> r q z w", r=PACK)
+            for r in range(PACK):
+                nc.sync.dma_start(out=plane[r:P:32], in_=rows[r])
+
+        for z in range(PASSES):
+            nc.sync.dma_start(out=xs_stage[z][:], in_=staged_rows(xt_scales, z))
+            nc.sync.dma_start(out=x_raw[z][:].bitcast(I32), in_=fp8_words(xt_words, z))
+            nc.sync.dma_start(out=wbs_stage[z][:], in_=staged_rows(wb_scales, z))
+            nc.sync.dma_start(out=wb_codes[z][:].bitcast(I32), in_=fp8_words(wb_words, z))
+        for side, weights in enumerate((ra, rb)):
+            nc.sync.dma_start(
+                out=r_block[:, side, :],
+                in_=weights.rearrange("o (g e) -> g o e", e=BLOCK).broadcast_to([T // BLOCK, RUN, BLOCK]),
+            )
+        load_plane(wa_plane[:].bitcast(I32), wa_scales)
+        nc.sync.dma_start(out=wa_codes[:].bitcast(I32), in_=wa_words.bitcast(I32).rearrange("z p w -> p z w"))
+        nc.sync.dma_start(out=sa_codes[:].bitcast(I32), in_=sa_words[0].bitcast(I32))
+        nc.sync.dma_start(out=sb_codes[:].bitcast(I32), in_=fp8_words(sb_words, 0))
+        load_plane(sa_plane[:].bitcast(I32).unsqueeze(1), sa_scales)
+        load_plane(sb_plane[:].bitcast(I32).unsqueeze(1), sb_scales)
+
+        for z in range(PASSES):
+            runs = x_raw[z][:].rearrange("p (g j i) -> p j g i", j=PACK, i=RUN)
+            for j in range(PACK):
+                nc.scalar.copy(out=x_codes[z][j][:].rearrange("p (g i) -> p g i", i=RUN), in_=runs[:, j])
+            for q in range(QUADS):
+                nc.vector.tensor_copy(
+                    out=x_plane[z][32 * q : 32 * q + PACK, :].rearrange("r (j g h) -> r j g h", j=PACK, h=2),
+                    in_=xs_stage[z][:, q, :].rearrange("r (g j h) -> r j g h", j=PACK, h=2),
+                )
+            for q in range(QUADS):
+                nc.vector.tensor_copy(out=wb_plane[z][32 * q : 32 * q + PACK, :], in_=wbs_stage[z][:, q, :])
+
+        nc.vector.tensor_scalar(out=lane_low[:], in0=lane[:], scalar1=RUN - 1, scalar2=None, op0=ALU.bitwise_and)
+        nc.vector.scalar_tensor_tensor(
+            out=r_picked[:].rearrange("p s i -> p (s i)"), in0=lane_low[:], scalar=0.0,
+            in1=r_block[:].rearrange("p s e -> p (s e)"), op0=ALU.is_equal, op1=ALU.mult,
+        )
+        nc.vector.tensor_reduce(
+            out=r_own[:].rearrange("p s j -> p (s j)"), in_=r_picked[:], axis=AXIS.X, op=ALU.add,
+        )
+
+        def layer_pass(acc, z, codes, plane):
+            x_bytes = x_plane[z][:].bitcast(U8)
+            for j in range(PACK):
+                nc.tensor.matmul_mx(
+                    out=acc[:, j, :],
+                    lhsT=x_codes[z][j][:].bitcast(FP8X4),
+                    lhsT_scale=x_bytes[:, j * P : (j + 1) * P],
+                    rhs=codes,
+                    rhs_scale=plane,
+                    start=(z == 0 and j == 0),
+                    stop=(z == PASSES - 1 and j == PACK - 1),
+                )
+
+        def b_pass(acc, c, z):
+            cols = slice(c * CHUNK, (c + 1) * CHUNK)
+            layer_pass(acc, z, wb_codes[z][:, cols].bitcast(FP8X4), wb_plane[z][:].bitcast(U8)[:, cols])
+
+        def a_pass(acc, c, z):
+            cols = slice(c * CHUNK, (c + 1) * CHUNK)
+            codes = wa_codes[:, z, 2 * c * CHUNK : 2 * (c + 1) * CHUNK].bitcast(FP4X4)
+            layer_pass(acc, z, codes, wa_plane[:, z, cols])
+
+        def token_weight(side):
+            return r_own[:, side, :].unsqueeze(1).broadcast_to([P, CHUNK, PACK])
+
+        def weigh_b(acc, c):
+            nc.vector.tensor_tensor(
+                out=bt[c // 2][:, (c % 2) * CHUNK : (c % 2 + 1) * CHUNK, :],
+                in0=acc[:].rearrange("p j m -> p m j"), in1=token_weight(1), op=ALU.mult,
+            )
+
+        def weigh_a(acc, c):
+            nc.vector.scalar_tensor_tensor(
+                out=at[c][:], in0=acc[:].rearrange("p j n -> p n j"), scalar=0.0, in1=token_weight(0),
+                op0=ALU.max, op1=ALU.mult,
+            )
+
+        def quantize_b(h):
+            cols = slice(h * 2 * CHUNK, (h + 1) * 2 * CHUNK)
+            nc.vector.quantize_mx(
+                out=bt_codes[:, cols].bitcast(FP8X4), scales=bt_plane[:, cols],
+                in_=bt[h][:].rearrange("p m j -> p (m j)"),
+            )
+
+        def quantize_a(c):
+            nc.vector.quantize_mx(
+                out=at_codes[c][:].bitcast(FP8X4), scales=at_plane[c][:],
+                in_=at[c][:].rearrange("p n j -> p (n j)"),
+            )
+
+        def stored_pass(acc, c, cols):
+            nc.tensor.matmul_mx(
+                out=acc[:],
+                lhsT=sa_codes[:, 2 * c * CHUNK : 2 * (c + 1) * CHUNK].bitcast(FP4X4),
+                lhsT_scale=sa_plane[:, c * CHUNK : (c + 1) * CHUNK],
+                rhs=sb_codes[:, cols].bitcast(FP8X4), rhs_scale=sb_plane[:, cols],
+                start=True, stop=False,
+            )
+
+        def token_pass(acc, c, cols):
+            nc.tensor.matmul_mx(
+                out=acc[:],
+                lhsT=at_codes[c][:].bitcast(FP8X4), lhsT_scale=at_plane[c][:],
+                rhs=bt_codes[:, cols].bitcast(FP8X4), rhs_scale=bt_plane[:, cols],
+                start=False, stop=True,
+            )
+
+        def whole_rows(c):
+            acc = bank(c, [P, M])
+            stored_pass(acc, c, slice(0, M))
+            token_pass(acc, c, slice(0, M))
+            result = sbuf("result%d" % c, [P, M], F32)
+            nc.scalar.activation(out=result[:], in_=acc[:], func=ACT.Copy, scale=OUT_SCALE)
+            nc.sync.dma_start(out=out[c * CHUNK : (c + 1) * CHUNK, :], in_=result[:])
+
+        b_acc = [bank(c, [P, PACK, CHUNK]) for c in range(CHUNKS)]
+        a_acc = [bank(CHUNKS + c, [P, PACK, CHUNK]) for c in range(CHUNKS)]
+
+        b_pass(b_acc[0], 0, 0)
+        b_pass(b_acc[1], 1, 0)
+        b_pass(b_acc[0], 0, 1)
+        weigh_b(b_acc[0], 0)
+        b_pass(b_acc[1], 1, 1)
+        weigh_b(b_acc[1], 1)
+        for c in (2, 3):
+            for z in range(PASSES):
+                b_pass(b_acc[c], c, z)
+            weigh_b(b_acc[c], c)
+            if c == 2:
+                quantize_b(0)
+        for c in range(CHUNKS):
+            if c == CHUNKS - 1:
+                whole_rows(0)
+            for z in range(PASSES):
+                a_pass(a_acc[c], c, z)
+            weigh_a(a_acc[c], c)
+            if c == 0:
+                quantize_b(1)
+            else:
+                quantize_a(c - 1)
+        last = CHUNKS - 1
+        quantize_a(last)
+        for c in range(1, last):
+            whole_rows(c)
+
+        halves = [slice(0, M // 2), slice(M // 2, M)]
+        half_acc = [bank(last + h, [P, M // 2]) for h in range(2)]
+        for h in range(2):
+            stored_pass(half_acc[h], last, halves[h])
+        rows = slice(last * CHUNK, (last + 1) * CHUNK)
+        half_result = [sbuf("half_result%d" % h, [P, M // 2], F32) for h in range(2)]
+        for h in range(2):
+            token_pass(half_acc[h], last, halves[h])
+        nc.vector.tensor_scalar(
+            out=half_result[0][:], in0=half_acc[0][:], scalar1=OUT_SCALE, scalar2=None, op0=ALU.mult,
+        )
+        nc.sync.dma_start(out=out[rows, halves[0]], in_=half_result[0][:])
+        nc.scalar.activation(out=half_result[1][:], in_=half_acc[1][:], func=ACT.Copy, scale=OUT_SCALE)
+        nc.scalar.dma_start(out=out[rows, halves[1]], in_=half_result[1][:])

@@ -26,6 +26,8 @@ RUN = 8
 BLOCK = 32
 OUT_SCALE = 0.04
 PLANE_WORDS = 128
+HALF = 64
+WB_ROW = 4
 
 
 def tile_mix_moment_of_two_layers_kernel(
@@ -46,11 +48,9 @@ def tile_mix_moment_of_two_layers_kernel(
 
         x_raw = [sbuf("x_raw%d" % z, [P, T], U32) for z in range(PASSES)]
         x_codes = [[sbuf("x_codes%d_%d" % (z, j), [P, P], U32) for j in range(PACK)] for z in range(PASSES)]
-        xs_stage = [sbuf("xs_stage%d" % z, [PACK, QUADS, PLANE_WORDS], I32) for z in range(PASSES)]
+        xw_rows = sbuf("xw_rows", [P, PASSES, 2, PLANE_WORDS], I32)
         x_plane = [sbuf("x_plane%d" % z, [P, PLANE_WORDS], I32) for z in range(PASSES)]
-        wb_codes = [sbuf("wb_codes%d" % z, [P, M], U32) for z in range(PASSES)]
-        wbs_stage = [sbuf("wbs_stage%d" % z, [PACK, QUADS, PLANE_WORDS], I32) for z in range(PASSES)]
-        wb_plane = [sbuf("wb_plane%d" % z, [P, PLANE_WORDS], I32) for z in range(PASSES)]
+        wb_codes = [sbuf("wb_codes%d" % h, [P, PASSES, M // 2], U32) for h in range(2)]
         wa_codes = sbuf("wa_codes", [P, PASSES, 2 * N], U8)
         wa_plane = sbuf("wa_plane", [P, PASSES, N], U8)
         sa_codes = sbuf("sa_codes", [P, 2 * N], U8)
@@ -69,35 +69,43 @@ def tile_mix_moment_of_two_layers_kernel(
         bt_codes = sbuf("bt_codes", [P, M], U32)
         bt_plane = sbuf("bt_plane", [P, M], U8)
 
-        for z in range(PASSES):
-            nc.vector.memset(x_plane[z][:], 0)
-            nc.vector.memset(wb_plane[z][:], 0)
+        nc.vector.memset(xw_rows[0:HALF], 0)
         nc.vector.memset(wa_plane[:].bitcast(I32), 0)
         nc.vector.memset(sa_plane[:].bitcast(I32), 0)
         nc.vector.memset(sb_plane[:].bitcast(I32), 0)
-        nc.gpsimd.iota(lane[:], pattern=[[0, 2 * PACK], [-1, RUN]], base=RUN, channel_multiplier=1)
 
         def fp8_words(words, z):
             return words[z].rearrange("p n t -> p (n t)").bitcast(I32)
 
-        def staged_rows(scales, z):
-            return scales[z].bitcast(I32).rearrange("(q r) w -> r q w", r=PACK)
+        def load_rows(first_row, scales, odd):
+            rows = scales.bitcast(I32).rearrange("z (h o r) w -> o r (z h) w", h=2, o=2)
+            first = 32 * odd + first_row
+            nc.sync.dma_start(
+                out=xw_rows[first : first + PACK].rearrange("r z h w -> r (z h) w"), in_=rows[odd],
+            )
+
+        def load_wb(h):
+            words = wb_words.rearrange("z p n t -> p z (n t)").bitcast(I32)
+            nc.sync.dma_start(out=wb_codes[h][:].bitcast(I32), in_=words[:, :, h * M // 2 : (h + 1) * M // 2])
 
         def load_plane(plane, scales):
             rows = scales.bitcast(I32).rearrange("z (q r) w -> r q z w", r=PACK)
             for r in range(PACK):
                 nc.sync.dma_start(out=plane[r:P:32], in_=rows[r])
 
-        for z in range(PASSES):
-            nc.sync.dma_start(out=xs_stage[z][:], in_=staged_rows(xt_scales, z))
-            nc.sync.dma_start(out=x_raw[z][:].bitcast(I32), in_=fp8_words(xt_words, z))
-            nc.sync.dma_start(out=wbs_stage[z][:], in_=staged_rows(wb_scales, z))
-            nc.sync.dma_start(out=wb_codes[z][:].bitcast(I32), in_=fp8_words(wb_words, z))
+        nc.gpsimd.iota(lane[:], pattern=[[0, 2 * PACK], [-1, RUN]], base=RUN, channel_multiplier=1)
+        nc.sync.dma_start(out=x_raw[0][:].bitcast(I32), in_=fp8_words(xt_words, 0))
+        for odd in range(2):
+            load_rows(0, xt_scales, odd)
+            load_rows(WB_ROW, wb_scales, odd)
+        load_wb(0)
         for side, weights in enumerate((ra, rb)):
             nc.sync.dma_start(
                 out=r_block[:, side, :],
                 in_=weights.rearrange("o (g e) -> g o e", e=BLOCK).broadcast_to([T // BLOCK, RUN, BLOCK]),
             )
+        nc.sync.dma_start(out=x_raw[1][:].bitcast(I32), in_=fp8_words(xt_words, 1))
+        load_wb(1)
         load_plane(wa_plane[:].bitcast(I32), wa_scales)
         nc.sync.dma_start(out=wa_codes[:].bitcast(I32), in_=wa_words.bitcast(I32).rearrange("z p w -> p z w"))
         nc.sync.dma_start(out=sa_codes[:].bitcast(I32), in_=sa_words[0].bitcast(I32))
@@ -105,19 +113,25 @@ def tile_mix_moment_of_two_layers_kernel(
         load_plane(sa_plane[:].bitcast(I32).unsqueeze(1), sa_scales)
         load_plane(sb_plane[:].bitcast(I32).unsqueeze(1), sb_scales)
 
-        for z in range(PASSES):
+        def reorder_words(z):
             runs = x_raw[z][:].rearrange("p (g j i) -> p j g i", j=PACK, i=RUN)
             for j in range(PACK):
                 nc.scalar.copy(out=x_codes[z][j][:].rearrange("p (g i) -> p g i", i=RUN), in_=runs[:, j])
-            for q in range(QUADS):
-                nc.vector.tensor_copy(
-                    out=x_plane[z][32 * q : 32 * q + PACK, :].rearrange("r (j g h) -> r j g h", j=PACK, h=2),
-                    in_=xs_stage[z][:, q, :].rearrange("r (g j h) -> r j g h", j=PACK, h=2),
-                )
-            for q in range(QUADS):
-                nc.vector.tensor_copy(out=wb_plane[z][32 * q : 32 * q + PACK, :], in_=wbs_stage[z][:, q, :])
+
+        def by_token(rows):
+            return rows.rearrange("r (g j h) -> r j g h", j=PACK, h=2)
+
+        def by_column(rows):
+            return rows.rearrange("r (j g h) -> r j g h", j=PACK, h=2)
 
         nc.vector.tensor_scalar(out=lane_low[:], in0=lane[:], scalar1=RUN - 1, scalar2=None, op0=ALU.bitwise_and)
+        reorder_words(0)
+        for z in range(PASSES):
+            nc.vector.tensor_copy(out=xw_rows[HALF:P, z, 0, :], in_=xw_rows[0:HALF, z, 1, :])
+        for z in range(PASSES):
+            nc.vector.tensor_copy(out=by_column(x_plane[z][:]), in_=by_token(xw_rows[:, z, 0, :]))
+        reorder_words(1)
+
         nc.vector.scalar_tensor_tensor(
             out=r_picked[:].rearrange("p s i -> p (s i)"), in0=lane_low[:], scalar=0.0,
             in1=r_block[:].rearrange("p s e -> p (s e)"), op0=ALU.is_equal, op1=ALU.mult,
@@ -141,7 +155,7 @@ def tile_mix_moment_of_two_layers_kernel(
 
         def b_pass(acc, c, z):
             cols = slice(c * CHUNK, (c + 1) * CHUNK)
-            layer_pass(acc, z, wb_codes[z][:, cols].bitcast(FP8X4), wb_plane[z][:].bitcast(U8)[:, cols])
+            layer_pass(acc, z, wb_codes[c // 2][:, z, (c % 2) * CHUNK : (c % 2 + 1) * CHUNK].bitcast(FP8X4), xw_rows[WB_ROW:P, z, 0, :].bitcast(U8)[:, cols])
 
         def a_pass(acc, c, z):
             cols = slice(c * CHUNK, (c + 1) * CHUNK)
@@ -204,21 +218,13 @@ def tile_mix_moment_of_two_layers_kernel(
         b_acc = [bank(c, [P, PACK, CHUNK]) for c in range(CHUNKS)]
         a_acc = [bank(CHUNKS + c, [P, PACK, CHUNK]) for c in range(CHUNKS)]
 
-        b_pass(b_acc[0], 0, 0)
-        b_pass(b_acc[1], 1, 0)
-        b_pass(b_acc[0], 0, 1)
-        weigh_b(b_acc[0], 0)
-        b_pass(b_acc[1], 1, 1)
-        weigh_b(b_acc[1], 1)
-        for c in (2, 3):
+        for c in range(CHUNKS):
             for z in range(PASSES):
                 b_pass(b_acc[c], c, z)
             weigh_b(b_acc[c], c)
             if c == 2:
                 quantize_b(0)
         for c in range(CHUNKS):
-            if c == CHUNKS - 1:
-                whole_rows(0)
             for z in range(PASSES):
                 a_pass(a_acc[c], c, z)
             weigh_a(a_acc[c], c)
@@ -228,7 +234,7 @@ def tile_mix_moment_of_two_layers_kernel(
                 quantize_a(c - 1)
         last = CHUNKS - 1
         quantize_a(last)
-        for c in range(1, last):
+        for c in range(last):
             whole_rows(c)
 
         halves = [slice(0, M // 2), slice(M // 2, M)]

@@ -47,7 +47,7 @@ def tile_mix_moment_of_two_layers_kernel(
             return ps.tile(shape, F32, name="bank%d" % index)
 
         x_raw = [sbuf("x_raw%d" % z, [P, T], U32) for z in range(PASSES)]
-        x_codes = [[sbuf("x_codes%d_%d" % (z, j), [P, P], U32) for j in range(PACK)] for z in range(PASSES)]
+        x_codes = [[sbuf("x_codes%d_%d" % (z, u), [P, 2 * P], U32) for u in range(2)] for z in range(PASSES)]
         xw_rows = sbuf("xw_rows", [P, PASSES, 2, PLANE_WORDS], I32)
         x_plane = [sbuf("x_plane%d" % z, [P, PLANE_WORDS], I32) for z in range(PASSES)]
         wb_codes = [sbuf("wb_codes%d" % h, [P, PASSES, M // 2], U32) for h in range(2)]
@@ -88,10 +88,9 @@ def tile_mix_moment_of_two_layers_kernel(
             words = wb_words.rearrange("z p n t -> p z (n t)").bitcast(I32)
             nc.sync.dma_start(out=wb_codes[h][:].bitcast(I32), in_=words[:, :, h * M // 2 : (h + 1) * M // 2])
 
-        def load_plane(plane, scales):
+        def load_plane_row(plane, scales, r):
             rows = scales.bitcast(I32).rearrange("z (q r) w -> r q z w", r=PACK)
-            for r in range(PACK):
-                nc.sync.dma_start(out=plane[r:P:32], in_=rows[r])
+            nc.sync.dma_start(out=plane[r:P:32], in_=rows[r])
 
         nc.gpsimd.iota(lane[:], pattern=[[0, 2 * PACK], [-1, RUN]], base=RUN, channel_multiplier=1)
         nc.sync.dma_start(out=x_raw[0][:].bitcast(I32), in_=fp8_words(xt_words, 0))
@@ -99,24 +98,31 @@ def tile_mix_moment_of_two_layers_kernel(
             load_rows(0, xt_scales, odd)
             load_rows(WB_ROW, wb_scales, odd)
         load_wb(0)
-        for side, weights in enumerate((ra, rb)):
+        nc.sync.dma_start(out=x_raw[1][:].bitcast(I32), in_=fp8_words(xt_words, 1))
+        load_wb(1)
+        for side, weights in ((1, rb), (0, ra)):
             nc.sync.dma_start(
                 out=r_block[:, side, :],
                 in_=weights.rearrange("o (g e) -> g o e", e=BLOCK).broadcast_to([T // BLOCK, RUN, BLOCK]),
             )
-        nc.sync.dma_start(out=x_raw[1][:].bitcast(I32), in_=fp8_words(xt_words, 1))
-        load_wb(1)
-        load_plane(wa_plane[:].bitcast(I32), wa_scales)
         nc.sync.dma_start(out=wa_codes[:].bitcast(I32), in_=wa_words.bitcast(I32).rearrange("z p w -> p z w"))
+        for r in range(PACK):
+            load_plane_row(wa_plane[:].bitcast(I32), wa_scales, r)
+        for r in range(2):
+            load_plane_row(sa_plane[:].bitcast(I32).unsqueeze(1), sa_scales, r)
         nc.sync.dma_start(out=sa_codes[:].bitcast(I32), in_=sa_words[0].bitcast(I32))
         nc.sync.dma_start(out=sb_codes[:].bitcast(I32), in_=fp8_words(sb_words, 0))
-        load_plane(sa_plane[:].bitcast(I32).unsqueeze(1), sa_scales)
-        load_plane(sb_plane[:].bitcast(I32).unsqueeze(1), sb_scales)
+        for r in range(2, PACK):
+            load_plane_row(sa_plane[:].bitcast(I32).unsqueeze(1), sa_scales, r)
+        for r in range(PACK):
+            load_plane_row(sb_plane[:].bitcast(I32).unsqueeze(1), sb_scales, r)
 
-        def reorder_words(z):
-            runs = x_raw[z][:].rearrange("p (g j i) -> p j g i", j=PACK, i=RUN)
-            for j in range(PACK):
-                nc.scalar.copy(out=x_codes[z][j][:].rearrange("p (g i) -> p g i", i=RUN), in_=runs[:, j])
+        def reorder_words(copy, dtype, z, u):
+            runs = x_raw[z][:].bitcast(dtype).rearrange("p (g j i) -> p j g i", j=PACK, i=RUN)
+            copy(
+                out=x_codes[z][u][:].bitcast(dtype).rearrange("p (j g i) -> p j g i", j=2, i=RUN),
+                in_=runs[:, 2 * u : 2 * u + 2],
+            )
 
         def by_token(rows):
             return rows.rearrange("r (g j h) -> r j g h", j=PACK, h=2)
@@ -125,12 +131,14 @@ def tile_mix_moment_of_two_layers_kernel(
             return rows.rearrange("r (j g h) -> r j g h", j=PACK, h=2)
 
         nc.vector.tensor_scalar(out=lane_low[:], in0=lane[:], scalar1=RUN - 1, scalar2=None, op0=ALU.bitwise_and)
-        reorder_words(0)
+        for u in range(2):
+            reorder_words(nc.scalar.copy, U32, 0, u)
         for z in range(PASSES):
             nc.vector.tensor_copy(out=xw_rows[HALF:P, z, 0, :], in_=xw_rows[0:HALF, z, 1, :])
         for z in range(PASSES):
             nc.vector.tensor_copy(out=by_column(x_plane[z][:]), in_=by_token(xw_rows[:, z, 0, :]))
-        reorder_words(1)
+        reorder_words(nc.scalar.copy, U32, 1, 0)
+        reorder_words(nc.vector.tensor_copy, I32, 1, 1)
 
         nc.vector.scalar_tensor_tensor(
             out=r_picked[:].rearrange("p s i -> p (s i)"), in0=lane_low[:], scalar=0.0,
@@ -145,7 +153,7 @@ def tile_mix_moment_of_two_layers_kernel(
             for j in range(PACK):
                 nc.tensor.matmul_mx(
                     out=acc[:, j, :],
-                    lhsT=x_codes[z][j][:].bitcast(FP8X4),
+                    lhsT=x_codes[z][j // 2][:, (j % 2) * P : (j % 2 + 1) * P].bitcast(FP8X4),
                     lhsT_scale=x_bytes[:, j * P : (j + 1) * P],
                     rhs=codes,
                     rhs_scale=plane,

@@ -27,6 +27,8 @@ BLOCK = 32
 OUT_SCALE = 0.04
 PLANE_WORDS = 128
 HALF = 64
+WARM_WIDTH = 256
+WARM_PASSES = (256, 256, 256, 256, 128)
 WB_ROW = 4
 
 
@@ -70,7 +72,12 @@ def tile_mix_moment_of_two_layers_kernel(
         bt_plane = sbuf("bt_plane", [P, M], U8)
 
         nc.vector.memset(xw_rows[0:HALF], 0)
+        warm_values = sbuf("warm_values", [P, PACK * WARM_WIDTH], BF16)
+        warm_codes = sbuf("warm_codes", [P, WARM_WIDTH], U32)
+        warm_plane = sbuf("warm_plane", [P, WARM_WIDTH], U8)
+        nc.vector.memset(warm_values[:].bitcast(I32), 0)
         nc.vector.memset(wa_plane[:].bitcast(I32), 0)
+        nc.vector.quantize_mx(out=warm_codes[:].bitcast(FP8X4), scales=warm_plane[:], in_=warm_values[:])
         nc.vector.memset(sa_plane[:].bitcast(I32), 0)
         nc.vector.memset(sb_plane[:].bitcast(I32), 0)
 
@@ -116,6 +123,15 @@ def tile_mix_moment_of_two_layers_kernel(
             load_plane_row(sa_plane[:].bitcast(I32).unsqueeze(1), sa_scales, r)
         for r in range(PACK):
             load_plane_row(sb_plane[:].bitcast(I32).unsqueeze(1), sb_scales, r)
+
+        warm_acc = bank(2 * CHUNKS - 1, [P, WARM_WIDTH])
+        for width in WARM_PASSES:
+            nc.tensor.matmul_mx(
+                out=warm_acc[:, 0:width],
+                lhsT=warm_codes[:, 0:P].bitcast(FP8X4), lhsT_scale=warm_plane[:, 0:P],
+                rhs=x_raw[0][:, 0:width].bitcast(FP8X4), rhs_scale=warm_plane[:, 0:width],
+                start=True, stop=True,
+            )
 
         def reorder_words(copy, dtype, z, u):
             runs = x_raw[z][:].bitcast(dtype).rearrange("p (g j i) -> p j g i", j=PACK, i=RUN)

from contextlib import ExitStack

import concourse.mybir as mybir

K, T, S, N, M = 1024, 512, 512, 512, 512
FLOPS = 2 * K * T * N + 2 * K * T * M + 2 * T * N * M + 2 * S * N * M

F32 = mybir.dt.float32
BF16 = mybir.dt.bfloat16
I32 = mybir.dt.int32
U32 = mybir.dt.uint32
U8 = mybir.dt.uint8
FP8X4 = mybir.dt.float8_e4m3fn_x4
FP4X4 = mybir.dt.float4_e2m1fn_x4
ALU = mybir.AluOpType
ACT = mybir.ActivationFunctionType
AXIS = mybir.AxisListType

P = 128
PACK = 4
PASSES = 2
QUADS = 4
CHUNK = 128
CHUNKS = 4
RUN = 8
BLOCK = 32
OUT_SCALE = 0.04
PLANE_WORDS = 128
HALF = 64
WARM_WIDTH = 256
WARM_PASSES = (256, 256, 256, 256, 128)
WB_ROW = 4


def tile_mix_moment_of_two_layers_kernel(
    tc, xt_words, xt_scales, wa_words, wa_scales, wb_words, wb_scales, ra, rb,
    sa_words, sa_scales, sb_words, sb_scales, out,
):
    nc = tc.nc
    with ExitStack() as ctx:
        sb = ctx.enter_context(tc.tile_pool(name="sb", bufs=1))
        ps = ctx.enter_context(tc.psum_pool(name="ps", bufs=1))
        ctx.enter_context(tc.manual_schedule())

        def sbuf(name, shape, dtype):
            return sb.tile(shape, dtype, name=name, align_bytes=64)

        def bank(index, shape):
            return ps.tile(shape, F32, name="bank%d" % index)

        x_raw = [sbuf("x_raw%d" % z, [P, T], U32) for z in range(PASSES)]
        x_codes = [[sbuf("x_codes%d_%d" % (z, u), [P, 2 * P], U32) for u in range(2)] for z in range(PASSES)]
        xw_rows = sbuf("xw_rows", [P, PASSES, 2, PLANE_WORDS], I32)
        x_plane = [sbuf("x_plane%d" % z, [P, PLANE_WORDS], I32) for z in range(PASSES)]
        wb_codes = [sbuf("wb_codes%d" % h, [P, PASSES, M // 2], U32) for h in range(2)]
        wa_codes = sbuf("wa_codes", [P, PASSES, 2 * N], U8)
        wa_plane = sbuf("wa_plane", [P, PASSES, N], U8)
        sa_codes = sbuf("sa_codes", [P, 2 * N], U8)
        sa_plane = sbuf("sa_plane", [P, N], U8)
        sb_codes = sbuf("sb_codes", [P, M], U32)
        sb_plane = sbuf("sb_plane", [P, M], U8)
        r_block = sbuf("r_block", [P, 2, BLOCK], F32)
        lane = sbuf("lane", [P, 2 * BLOCK], I32)
        lane_low = sbuf("lane_low", [P, 2 * BLOCK], I32)
        r_picked = sbuf("r_picked", [P, 2 * PACK, RUN], F32)
        r_own = sbuf("r_own", [P, 2, PACK], F32)
        at = [sbuf("at%d" % c, [P, CHUNK, PACK], BF16) for c in range(CHUNKS)]
        bt = [sbuf("bt%d" % h, [P, 2 * CHUNK, PACK], BF16) for h in range(2)]
        at_codes = [sbuf("at_codes%d" % c, [P, CHUNK], U32) for c in range(CHUNKS)]
        at_plane = [sbuf("at_plane%d" % c, [P, CHUNK], U8) for c in range(CHUNKS)]
        bt_codes = sbuf("bt_codes", [P, M], U32)
        bt_plane = sbuf("bt_plane", [P, M], U8)

        nc.vector.memset(xw_rows[0:HALF], 0)
        warm_values = sbuf("warm_values", [P, PACK * WARM_WIDTH], BF16)
        warm_codes = sbuf("warm_codes", [P, WARM_WIDTH], U32)
        warm_plane = sbuf("warm_plane", [P, WARM_WIDTH], U8)
        nc.vector.memset(warm_values[:].bitcast(I32), 0)
        nc.vector.memset(wa_plane[:].bitcast(I32), 0)
        nc.vector.quantize_mx(out=warm_codes[:].bitcast(FP8X4), scales=warm_plane[:], in_=warm_values[:])
        nc.vector.memset(sa_plane[:].bitcast(I32), 0)
        nc.vector.memset(sb_plane[:].bitcast(I32), 0)

        def fp8_words(words, z):
            return words[z].rearrange("p n t -> p (n t)").bitcast(I32)

        def load_rows(first_row, scales, odd):
            rows = scales.bitcast(I32).rearrange("z (h o r) w -> o r (z h) w", h=2, o=2)
            first = 32 * odd + first_row
            nc.sync.dma_start(
                out=xw_rows[first : first + PACK].rearrange("r z h w -> r (z h) w"), in_=rows[odd],
            )

        def load_wb(h):
            words = wb_words.rearrange("z p n t -> p z (n t)").bitcast(I32)
            nc.sync.dma_start(out=wb_codes[h][:].bitcast(I32), in_=words[:, :, h * M // 2 : (h + 1) * M // 2])

        def load_plane_row(plane, scales, r):
            rows = scales.bitcast(I32).rearrange("z (q r) w -> r q z w", r=PACK)
            nc.sync.dma_start(out=plane[r:P:32], in_=rows[r])

        nc.gpsimd.iota(lane[:], pattern=[[0, 2 * PACK], [-1, RUN]], base=RUN, channel_multiplier=1)
        nc.sync.dma_start(out=x_raw[0][:].bitcast(I32), in_=fp8_words(xt_words, 0))
        for odd in range(2):
            load_rows(0, xt_scales, odd)
            load_rows(WB_ROW, wb_scales, odd)
        load_wb(0)
        nc.sync.dma_start(out=x_raw[1][:].bitcast(I32), in_=fp8_words(xt_words, 1))
        load_wb(1)
        for side, weights in ((1, rb), (0, ra)):
            nc.sync.dma_start(
                out=r_block[:, side, :],
                in_=weights.rearrange("o (g e) -> g o e", e=BLOCK).broadcast_to([T // BLOCK, RUN, BLOCK]),
            )
        nc.sync.dma_start(out=wa_codes[:].bitcast(I32), in_=wa_words.bitcast(I32).rearrange("z p w -> p z w"))
        for r in range(PACK):
            load_plane_row(wa_plane[:].bitcast(I32), wa_scales, r)
        for r in range(2):
            load_plane_row(sa_plane[:].bitcast(I32).unsqueeze(1), sa_scales, r)
        nc.sync.dma_start(out=sa_codes[:].bitcast(I32), in_=sa_words[0].bitcast(I32))
        nc.sync.dma_start(out=sb_codes[:].bitcast(I32), in_=fp8_words(sb_words, 0))
        for r in range(2, PACK):
            load_plane_row(sa_plane[:].bitcast(I32).unsqueeze(1), sa_scales, r)
        for r in range(PACK):
            load_plane_row(sb_plane[:].bitcast(I32).unsqueeze(1), sb_scales, r)

        warm_acc = bank(2 * CHUNKS - 1, [P, WARM_WIDTH])
        for width in WARM_PASSES:
            nc.tensor.matmul_mx(
                out=warm_acc[:, 0:width],
                lhsT=warm_codes[:, 0:P].bitcast(FP8X4), lhsT_scale=warm_plane[:, 0:P],
                rhs=x_raw[0][:, 0:width].bitcast(FP8X4), rhs_scale=warm_plane[:, 0:width],
                start=True, stop=True,
            )

        def reorder_words(copy, dtype, z, u):
            runs = x_raw[z][:].bitcast(dtype).rearrange("p (g j i) -> p j g i", j=PACK, i=RUN)
            copy(
                out=x_codes[z][u][:].bitcast(dtype).rearrange("p (j g i) -> p j g i", j=2, i=RUN),
                in_=runs[:, 2 * u : 2 * u + 2],
            )

        def by_token(rows):
            return rows.rearrange("r (g j h) -> r j g h", j=PACK, h=2)

        def by_column(rows):
            return rows.rearrange("r (j g h) -> r j g h", j=PACK, h=2)

        nc.vector.tensor_scalar(out=lane_low[:], in0=lane[:], scalar1=RUN - 1, scalar2=None, op0=ALU.bitwise_and)
        for u in range(2):
            reorder_words(nc.scalar.copy, U32, 0, u)
        for z in range(PASSES):
            nc.vector.tensor_copy(out=xw_rows[HALF:P, z, 0, :], in_=xw_rows[0:HALF, z, 1, :])
        for z in range(PASSES):
            nc.vector.tensor_copy(out=by_column(x_plane[z][:]), in_=by_token(xw_rows[:, z, 0, :]))
        reorder_words(nc.scalar.copy, U32, 1, 0)
        reorder_words(nc.vector.tensor_copy, I32, 1, 1)

        nc.vector.scalar_tensor_tensor(
            out=r_picked[:].rearrange("p s i -> p (s i)"), in0=lane_low[:], scalar=0.0,
            in1=r_block[:].rearrange("p s e -> p (s e)"), op0=ALU.is_equal, op1=ALU.mult,
        )
        nc.vector.tensor_reduce(
            out=r_own[:].rearrange("p s j -> p (s j)"), in_=r_picked[:], axis=AXIS.X, op=ALU.add,
        )

        def layer_pass(acc, z, codes, plane):
            x_bytes = x_plane[z][:].bitcast(U8)
            for j in range(PACK):
                nc.tensor.matmul_mx(
                    out=acc[:, j, :],
                    lhsT=x_codes[z][j // 2][:, (j % 2) * P : (j % 2 + 1) * P].bitcast(FP8X4),
                    lhsT_scale=x_bytes[:, j * P : (j + 1) * P],
                    rhs=codes,
                    rhs_scale=plane,
                    start=(z == 0 and j == 0),
                    stop=(z == PASSES - 1 and j == PACK - 1),
                )

        def b_pass(acc, c, z):
            cols = slice(c * CHUNK, (c + 1) * CHUNK)
            layer_pass(acc, z, wb_codes[c // 2][:, z, (c % 2) * CHUNK : (c % 2 + 1) * CHUNK].bitcast(FP8X4), xw_rows[WB_ROW:P, z, 0, :].bitcast(U8)[:, cols])

        def a_pass(acc, c, z):
            cols = slice(c * CHUNK, (c + 1) * CHUNK)
            codes = wa_codes[:, z, 2 * c * CHUNK : 2 * (c + 1) * CHUNK].bitcast(FP4X4)
            layer_pass(acc, z, codes, wa_plane[:, z, cols])

        def token_weight(side):
            return r_own[:, side, :].unsqueeze(1).broadcast_to([P, CHUNK, PACK])

        def weigh_b(acc, c):
            nc.vector.tensor_tensor(
                out=bt[c // 2][:, (c % 2) * CHUNK : (c % 2 + 1) * CHUNK, :],
                in0=acc[:].rearrange("p j m -> p m j"), in1=token_weight(1), op=ALU.mult,
            )

        def weigh_a(acc, c):
            nc.vector.scalar_tensor_tensor(
                out=at[c][:], in0=acc[:].rearrange("p j n -> p n j"), scalar=0.0, in1=token_weight(0),
                op0=ALU.max, op1=ALU.mult,
            )

        def quantize_b(h):
            cols = slice(h * 2 * CHUNK, (h + 1) * 2 * CHUNK)
            nc.vector.quantize_mx(
                out=bt_codes[:, cols].bitcast(FP8X4), scales=bt_plane[:, cols],
                in_=bt[h][:].rearrange("p m j -> p (m j)"),
            )

        def quantize_a(c):
            nc.vector.quantize_mx(
                out=at_codes[c][:].bitcast(FP8X4), scales=at_plane[c][:],
                in_=at[c][:].rearrange("p n j -> p (n j)"),
            )

        def stored_pass(acc, c, cols):
            nc.tensor.matmul_mx(
                out=acc[:],
                lhsT=sa_codes[:, 2 * c * CHUNK : 2 * (c + 1) * CHUNK].bitcast(FP4X4),
                lhsT_scale=sa_plane[:, c * CHUNK : (c + 1) * CHUNK],
                rhs=sb_codes[:, cols].bitcast(FP8X4), rhs_scale=sb_plane[:, cols],
                start=True, stop=False,
            )

        def token_pass(acc, c, cols):
            nc.tensor.matmul_mx(
                out=acc[:],
                lhsT=at_codes[c][:].bitcast(FP8X4), lhsT_scale=at_plane[c][:],
                rhs=bt_codes[:, cols].bitcast(FP8X4), rhs_scale=bt_plane[:, cols],
                start=False, stop=True,
            )

        def whole_rows(c):
            acc = bank(c, [P, M])
            stored_pass(acc, c, slice(0, M))
            token_pass(acc, c, slice(0, M))
            result = sbuf("result%d" % c, [P, M], F32)
            nc.scalar.activation(out=result[:], in_=acc[:], func=ACT.Copy, scale=OUT_SCALE)
            nc.sync.dma_start(out=out[c * CHUNK : (c + 1) * CHUNK, :], in_=result[:])

        b_acc = [bank(c, [P, PACK, CHUNK]) for c in range(CHUNKS)]
        a_acc = [bank(CHUNKS + c, [P, PACK, CHUNK]) for c in range(CHUNKS)]

        for c in range(CHUNKS):
            for z in range(PASSES):
                b_pass(b_acc[c], c, z)
            weigh_b(b_acc[c], c)
            if c == 2:
                quantize_b(0)
        for c in range(CHUNKS):
            for z in range(PASSES):
                a_pass(a_acc[c], c, z)
            weigh_a(a_acc[c], c)
            if c == 0:
                quantize_b(1)
            else:
                quantize_a(c - 1)
        last = CHUNKS - 1
        quantize_a(last)
        for c in range(last):
            whole_rows(c)

        halves = [slice(0, M // 2), slice(M // 2, M)]
        half_acc = [bank(last + h, [P, M // 2]) for h in range(2)]
        for h in range(2):
            stored_pass(half_acc[h], last, halves[h])
        rows = slice(last * CHUNK, (last + 1) * CHUNK)
        half_result = [sbuf("half_result%d" % h, [P, M // 2], F32) for h in range(2)]
        for h in range(2):
            token_pass(half_acc[h], last, halves[h])
        nc.vector.tensor_scalar(
            out=half_result[0][:], in0=half_acc[0][:], scalar1=OUT_SCALE, scalar2=None, op0=ALU.mult,
        )
        nc.sync.dma_start(out=out[rows, halves[0]], in_=half_result[0][:])
        nc.scalar.activation(out=half_result[1][:], in_=half_acc[1][:], func=ACT.Copy, scale=OUT_SCALE)
        nc.scalar.dma_start(out=out[rows, halves[1]], in_=half_result[1][:])
